import numpy as np
import ml_dtypes


def mxq(x, axis, fmt="e4m3"):
    dtype, down = {"e4m3": (ml_dtypes.float8_e4m3fn, 7), "e5m2": (ml_dtypes.float8_e5m2, 14)}[fmt]
    v = np.moveaxis(np.asarray(x, np.float32).astype(ml_dtypes.bfloat16).astype(np.float64), axis, -1)
    blocks = v.reshape(v.shape[:-1] + (-1, 32))
    amax = np.abs(blocks).max(-1, keepdims=True)
    byte = np.maximum(np.where(amax > 0, np.frexp(amax)[1] - 1 + 127, 0) - down, 1)
    scale = np.exp2(byte - 127.0)
    codes = (blocks / scale).astype(np.float32).astype(dtype).astype(np.float64)
    return np.moveaxis((codes * scale).reshape(v.shape), -1, axis)


WIDE = False


def mx_kscale(k):
    if not WIDE:
        return np.ones(k)
    levels = np.array([10, -10, 5, -5, 0])
    if k % 512:
        return np.exp2(np.random.permutation(np.resize(levels, k // 32))).repeat(32)
    a = np.empty((k // 512, 16))
    for p in range(k // 512):
        a[p, :8] = np.random.permutation(np.resize(levels, 8))
        for g in range(8):
            far = levels[np.abs(levels - a[p, g]) >= 10]
            a[p, g + 8] = far[np.random.randint(len(far))]
    return np.exp2(a.ravel()).repeat(32)


def f64(x):
    return np.asarray(x).astype(np.float64)


def striped(idx):
    return np.tile(idx.reshape(-1, 16).T, (8, 1)).astype(np.uint16)


def unstriped(offs):
    return offs[:16].T.reshape(-1).astype(np.int64)


def pack_weight(w):
    k, n = w.shape
    w = f64(np.asarray(w, np.float32).astype(ml_dtypes.bfloat16)).reshape(k // 32, 32, n)
    amax = np.abs(w).max(1)
    byte = np.clip(np.where(amax > 0, np.frexp(amax)[1] - 1 + 127 - 7, 1), 1, 254)
    scaled = (w * np.exp2(127.0 - byte)[:, None, :]).reshape(k, n).astype(np.float32)
    words = np.ascontiguousarray(scaled.reshape(k // 512, 128, 4, n).transpose(0, 1, 3, 2)).astype(ml_dtypes.float8_e4m3fn).view(np.uint8)
    return words, np.ascontiguousarray(byte.astype(np.uint8).reshape(k // 512, 16, n))


def unpack_weight(words, scales):
    g, p, n, _ = words.shape
    vals = np.ascontiguousarray(words).view(ml_dtypes.float8_e4m3fn).astype(np.float64) * np.repeat(np.exp2(scales.astype(np.float64) - 127.0), 8, axis=1)[..., None]
    return vals.transpose(0, 1, 3, 2).reshape(g * 512, n)


def relu(v):
    return np.maximum(v, 0.0)


K, T, S, D, N, H = 512, 2048, 1024, 2, 256, 512


def setup_inputs():
    n = np.random.standard_normal
    s = mx_kscale(K)[:, None]
    u = mx_kscale(H)
    packed_xT = pack_weight(n((K, T)) * s)
    return {
        "x_words": packed_xT[0],
        "x_scales": packed_xT[1],
        "w1": (n((K, H)) / np.sqrt(K) / s).astype(np.float32),
        "w2": (n((K, H)) / np.sqrt(K) / s).astype(np.float32),
        "infl": (np.random.uniform(0.5, 2.0, (H, S))).astype(np.float32),
        "unit": (np.random.uniform(0.6, 1.4, (H, 1)) * u[:, None]).astype(np.float32),
        "w3": (n((H, N)) / np.sqrt(H) / u[:, None]).astype(np.float32),
        "offs": striped(np.random.permutation(T)[:S]),
        "shr": striped(np.random.permutation(S)),
    }


def reference(x_words, x_scales, w1, w2, infl, unit, w3, offs, shr):
    xq = unpack_weight(x_words, x_scales)[:, unstriped(offs)]
    bw = mxq(f64(w1), 0, "e4m3").T @ xq
    btl = np.log(np.exp(bw) + 1.0)
    rt = mxq(f64(w2), 0, "e4m3").T @ xq
    rtt = np.log(np.exp(rt) + 1.0) + 0.3
    bdp = btl * rtt
    que = relu(f64(infl) - (0.7 * bdp))
    qs = que[:, unstriped(shr)]
    bs = btl[:, unstriped(shr)]
    pace = (btl * (qs + 0.5)) / (que + bs + 0.5)
    pairsum = np.repeat(pace.reshape(len(pace), -1, D).sum(axis=2), D, axis=1)
    hid = f64(unit) * (pace - (0.3 * pairsum))
    return mxq(f64(w3), 0, "e4m3").T @ mxq(hid, 0, "e4m3")

@@ -1,0 +1,247 @@
+from contextlib import ExitStack
+
+import concourse.mybir as mybir
+from concourse.masks import make_identity
+
+K, T, S, N, H = 512, 2048, 1024, 256, 512
+FLOPS = 2 * K * H * S * 2 + 2 * H * N * S
+
+F32 = mybir.dt.float32
+BF16 = mybir.dt.bfloat16
+I32 = mybir.dt.int32
+U32 = mybir.dt.uint32
+U16 = mybir.dt.uint16
+U8 = mybir.dt.uint8
+FP8X4 = mybir.dt.float8_e4m3fn_x4
+ALU = mybir.AluOpType
+ACT = mybir.ActivationFunctionType
+
+P = 128
+PACK = 4
+HALF = 512
+PAIRS = HALF // 2
+COLS = HALF // 16
+LN_FLOOR = 2.0 ** -60
+
+
+def tile_picked_ytcpcc_pace_p_kernel(
+    tc, x_words, x_scales, w1, w2, infl, unit, w3, offs, shr, out
+):
+    nc = tc.nc
+    with ExitStack() as ctx:
+        keep = ctx.enter_context(tc.tile_pool(name="keep", bufs=1))
+        psum = ctx.enter_context(tc.psum_pool(name="psum", bufs=1))
+
+        def sb(name, shape, dtype, tag=None):
+            return keep.tile(shape, dtype, name=name, tag=tag or name, align_bytes=64)
+
+        offs_sb = sb("offs_sb", [P, S // 16], U16)
+        shr_sb = sb("shr_sb", [P, S // 16], U16)
+        xw = sb("xw", [P, T], U32)
+        xs = sb("xs", [P, T], U8)
+        nc.vector.memset(xs[:].bitcast(I32), 0)
+        nc.sync.dma_start(offs_sb[:], offs)
+        nc.sync.dma_start(
+            xw[:].bitcast(I32), x_words[0].rearrange("p n t -> p (n t)").bitcast(I32)
+        )
+        for q in range(4):
+            nc.sync.dma_start(
+                xs[32 * q : 32 * q + 4, :].bitcast(I32),
+                x_scales[0][4 * q : 4 * q + 4, :].bitcast(I32),
+            )
+        w_raw = []
+        for name, w in (("w1", w1), ("w2", w2)):
+            raw = sb(name + "_raw", [P, PACK, H], F32)
+            nc.sync.dma_start(raw[:], w.rearrange("(p j) c -> p j c", j=PACK))
+            w_raw.append(raw)
+        nc.sync.dma_start(shr_sb[:], shr)
+        infl_rows = infl.rearrange("(p t) j -> p t j", t=PACK)
+        infl_sb = []
+        for t in range(PACK):
+            tile = sb("infl%d" % t, [P, S], F32)
+            nc.sync.dma_start(tile[:], infl_rows[:, t, :])
+            infl_sb.append(tile)
+        unit_sb = sb("unit_sb", [P, PACK], F32)
+        nc.sync.dma_start(unit_sb[:], unit.rearrange("(p t) o -> p (t o)", t=PACK))
+        w3_raw = sb("w3_raw", [P, PACK, N], F32)
+        nc.sync.dma_start(w3_raw[:], w3.rearrange("(p j) c -> p j c", j=PACK))
+
+        ident = sb("ident", [P, P], F32)
+        make_identity(nc, ident[:])
+
+        gw, gs = {}, {}
+        w_codes, w_scales = {}, {}
+
+        def pick(h):
+            gw[h] = sb("gw%d" % h, [P, HALF], U32, tag="gw%d" % h)
+            gs[h] = sb("gs%d" % h, [P, HALF], U8)
+            sl = offs_sb[:, h * COLS : (h + 1) * COLS]
+            nc.vector.tensor_copy(gw[h][:], xw[:].indirect(sl))
+            nc.vector.tensor_copy(gs[h][:], xs[:].indirect(sl))
+
+        def weights(i, g):
+            tag = "gw1" if (i, g) == (0, 0) else "wg%d_%d" % (i, g)
+            grouped = sb("wg%d_%d" % (i, g), [P, 2 * P * PACK], BF16, tag=tag)
+            nc.vector.tensor_copy(
+                grouped[:].rearrange("p (t m j) -> p m t j", t=2, j=PACK),
+                w_raw[i][:].rearrange("p j (m t) -> p m t j", t=PACK)[:, :, 2 * g : 2 * g + 2, :],
+            )
+            w_codes[i, g] = sb("wc%d_%d" % (i, g), [P, 2 * P], U32)
+            w_scales[i, g] = sb("ws%d_%d" % (i, g), [P, 2 * P], U8)
+            nc.vector.quantize_mx(out=w_codes[i, g][:].bitcast(FP8X4), scales=w_scales[i, g][:], in_=grouped[:])
+
+        pick(0)
+        weights(0, 0)
+        pick(1)
+        weights(1, 0)
+        weights(0, 1)
+        weights(1, 1)
+
+        w3g = sb("w3g", [P, N * PACK], BF16)
+        nc.vector.tensor_copy(
+            w3g[:].rearrange("p (c j) -> p c j", j=PACK), w3_raw[:].rearrange("p j c -> p c j")
+        )
+        w3_codes = sb("w3c", [P, N], U32)
+        w3_scales = sb("w3s", [P, N], U8)
+        nc.vector.quantize_mx(out=w3_codes[:].bitcast(FP8X4), scales=w3_scales[:], in_=w3g[:])
+        unit7 = sb("unit7", [P, PACK], F32)
+        nc.vector.tensor_scalar_mul(unit7[:], unit_sb[:], 0.7)
+
+        halves = [slice(h * HALF, (h + 1) * HALF) for h in range(2)]
+        btl = [sb("btl%d" % t, [P, S], F32) for t in range(PACK)]
+        q5 = [sb("q5_%d" % t, [P, S], F32) for t in range(PACK)]
+        work = [sb("work%d" % t, [P, S], F32) for t in range(PACK)]
+        num = [sb("num%d" % t, [P, S], F32) for t in range(PACK)]
+        den = [sb("den%d" % t, [P, S], F32) for t in range(PACK)]
+        pace = [sb("pace%d" % g, [P, 2, S], F32) for g in range(2)]
+        pairw = [sb("pairw%d" % h, [P, 2, 2, PAIRS, 2], BF16) for h in range(2)]
+
+        def softplus(g):
+            ts = (2 * g, 2 * g + 1)
+            banks, sig = {}, {}
+            for t in ts:
+                for h in range(2):
+                    sig[t, h] = sb("sig%d_%d" % (t, h), [P, 2, HALF], F32, tag="sig%d_%d" % (t % 2, h))
+            for i in range(2):
+                for t in ts:
+                    for h in range(2):
+                        bank = psum.tile([P, HALF], F32, name="acc", tag="bank%d" % (4 * (t % 2) + 2 * h + i))
+                        cols = slice((t % 2) * P, (t % 2 + 1) * P)
+                        nc.tensor.matmul_mx(
+                            out=bank[:],
+                            lhsT=w_codes[i, g][:, cols].bitcast(FP8X4),
+                            lhsT_scale=w_scales[i, g][:, cols],
+                            rhs=gw[h][:].bitcast(FP8X4),
+                            rhs_scale=gs[h][:],
+                            start=True,
+                            stop=True,
+                        )
+                        nc.scalar.activation(sig[t, h][:, i, :], bank[:], ACT.Sigmoid, scale=-1.0)
+                        banks[i, t, h] = bank
+            for t in ts:
+                for h in range(2):
+                    nc.scalar.activation(sig[t, h][:], sig[t, h][:], ACT.Ln, bias=LN_FLOOR)
+                    for i, dst in enumerate((btl, work)):
+                        nc.vector.scalar_tensor_tensor(
+                            dst[t][:, halves[h]], sig[t, h][:, i, :], -1.0, banks[i, t, h][:], ALU.mult, ALU.max
+                        )
+
+        def queue(g):
+            ts = (2 * g, 2 * g + 1)
+            for t in ts:
+                nc.vector.scalar_tensor_tensor(work[t][:], work[t][:], 0.3, btl[t][:], ALU.add, ALU.mult)
+            for t in ts:
+                nc.vector.scalar_tensor_tensor(work[t][:], work[t][:], -0.7, infl_sb[t][:], ALU.mult, ALU.add)
+            for t in ts:
+                nc.vector.tensor_scalar(q5[t][:], work[t][:], 0.0, 0.5, ALU.max, ALU.add)
+
+        def shared_btl(t, h):
+            sl = shr_sb[:, h * COLS : (h + 1) * COLS]
+            nc.scalar.activation(den[t][:, halves[h]], btl[t][:].indirect(sl), ACT.Copy)
+
+        def numerator(t, h):
+            sl = shr_sb[:, h * COLS : (h + 1) * COLS]
+            nc.vector.tensor_tensor(num[t][:, halves[h]], q5[t][:].indirect(sl), btl[t][:, halves[h]], ALU.mult)
+
+        back = {}
+
+        def invert(t, h):
+            turned = psum.tile([P, HALF], F32, name="turned", tag="bank%d" % (2 * (t % 2) + h))
+            for c in range(HALF // P):
+                src = slice(h * HALF + c * P, h * HALF + (c + 1) * P)
+                dst = turned[:, c * P : (c + 1) * P]
+                nc.tensor.matmul(dst, den[t][:, src], ident[:], start=True, stop=False, is_transpose=True)
+                nc.tensor.matmul(dst, q5[t][:, src], ident[:], start=False, stop=True, is_transpose=True)
+            root = sb("root%d_%d" % (t, h), [P, HALF], F32)
+            nc.scalar.activation(root[:], turned[:], ACT.Abs_reciprocal_sqrt)
+            nc.scalar.activation(root[:], root[:], ACT.Square)
+            back[t, h] = psum.tile([P, HALF], F32, name="back", tag="bank%d" % (4 + 2 * (t % 2) + h))
+            for c in range(HALF // P):
+                blk = slice(c * P, (c + 1) * P)
+                nc.tensor.transpose(back[t, h][:, blk], root[:, blk], ident[:])
+
+        def paces(t, h):
+            nc.vector.scalar_tensor_tensor(
+                pace[t // 2][:, t % 2, halves[h]], num[t][:, halves[h]], unit7[:, t : t + 1], back[t, h][:],
+                ALU.mult, ALU.mult,
+            )
+
+        def pair(g, h):
+            members = pace[g][:, :, halves[h]].rearrange("p t (v d) -> p d v t", d=2)
+            for d in range(2):
+                nc.vector.scalar_tensor_tensor(
+                    pairw[h][:, g, d, :, :], members[:, 1 - d, :, :], -3.0 / 7.0, members[:, d, :, :],
+                    ALU.mult, ALU.add,
+                )
+
+        def finish(h):
+            hid = sb("hid%d" % h, [P, HALF * PACK], BF16)
+            nc.vector.tensor_copy(
+                hid[:].bitcast(I32).rearrange("p (c g) -> p c g", g=2),
+                pairw[h][:].rearrange("p g d v t -> p (g d v t)").bitcast(I32).rearrange("p (g c) -> p c g", g=2),
+            )
+            codes = sb("hc%d" % h, [P, HALF], U32)
+            scales = sb("hs%d" % h, [P, HALF], U8)
+            nc.vector.quantize_mx(out=codes[:].bitcast(FP8X4), scales=scales[:], in_=hid[:])
+            for m in range(N // P):
+                bank = psum.tile([P, HALF], F32, name="acc_out", tag="bank%d" % (2 * h + m))
+                cols = slice(m * P, (m + 1) * P)
+                nc.tensor.matmul_mx(
+                    out=bank[:],
+                    lhsT=w3_codes[:, cols].bitcast(FP8X4),
+                    lhsT_scale=w3_scales[:, cols],
+                    rhs=codes[:].bitcast(FP8X4),
+                    rhs_scale=scales[:],
+                    start=True,
+                    stop=True,
+                )
+                res = sb("res%d_%d" % (h, m), [P, HALF], F32)
+                nc.scalar.copy(
+                    res[:].rearrange("p (v d) -> p v d", d=2), bank[:].rearrange("p (d v) -> p v d", d=2)
+                )
+                nc.sync.dma_start(out[cols, halves[h]], res[:])
+
+        def each(f, g):
+            for h in range(2):
+                for t in (2 * g, 2 * g + 1):
+                    f(t, h)
+
+        softplus(0)
+        softplus(1)
+        queue(0)
+        each(numerator, 0)
+        each(shared_btl, 0)
+        queue(1)
+        each(invert, 0)
+        each(shared_btl, 1)
+        each(numerator, 1)
+        each(paces, 0)
+        pair(0, 0)
+        pair(0, 1)
+        each(invert, 1)
+        for h in range(2):
+            paces(2, h)
+            paces(3, h)
+        for h in range(2):
+            pair(1, h)
+            finish(h)

@@ -80,11 +80,11 @@ def tile_picked_ytcpcc_pace_p_kernel(
             nc.vector.tensor_copy(gs[h][:], xs[:].indirect(sl))
 
         def weights(i, g):
-            tag = "gw1" if (i, g) == (0, 0) else "wg%d_%d" % (i, g)
+            tag = "gw1" if (i, g) == (0, 0) else "wg"
             grouped = sb("wg%d_%d" % (i, g), [P, 2 * P * PACK], BF16, tag=tag)
             nc.vector.tensor_copy(
-                grouped[:].rearrange("p (t m j) -> p m t j", t=2, j=PACK),
-                w_raw[i][:].rearrange("p j (m t) -> p m t j", t=PACK)[:, :, 2 * g : 2 * g + 2, :],
+                grouped[:].rearrange("p (t m j) -> p m j t", t=2, j=PACK),
+                w_raw[i][:].rearrange("p j (m t) -> p m j t", t=PACK)[:, :, :, 2 * g : 2 * g + 2],
             )
             w_codes[i, g] = sb("wc%d_%d" % (i, g), [P, 2 * P], U32)
             w_scales[i, g] = sb("ws%d_%d" % (i, g), [P, 2 * P], U8)
@@ -99,7 +99,8 @@ def tile_picked_ytcpcc_pace_p_kernel(
 
         w3g = sb("w3g", [P, N * PACK], BF16)
         nc.vector.tensor_copy(
-            w3g[:].rearrange("p (c j) -> p c j", j=PACK), w3_raw[:].rearrange("p j c -> p c j")
+            w3g[:].rearrange("p (c i j) -> p c j i", i=4, j=PACK),
+            w3_raw[:].rearrange("p j (c i) -> p c j i", i=4),
         )
         w3_codes = sb("w3c", [P, N], U32)
         w3_scales = sb("w3s", [P, N], U8)
@@ -113,8 +114,9 @@ def tile_picked_ytcpcc_pace_p_kernel(
         work = [sb("work%d" % t, [P, S], F32) for t in range(PACK)]
         num = [sb("num%d" % t, [P, S], F32) for t in range(PACK)]
         den = [sb("den%d" % t, [P, S], F32) for t in range(PACK)]
-        pace = [sb("pace%d" % g, [P, 2, S], F32) for g in range(2)]
-        pairw = [sb("pairw%d" % h, [P, 2, 2, PAIRS, 2], BF16) for h in range(2)]
+        pace = {(g, h): sb("pace%d_%d" % (g, h), [P, 2, HALF], F32) for g in range(2) for h in range(2)}
+        pieces = ((0, 512), (512, 256), (768, 256))
+        pairw = [sb("pairw%d" % k, [P, 2, 2, w // 2, 2], BF16) for k, (c0, w) in enumerate(pieces)]
 
         def softplus(g):
             ts = (2 * g, 2 * g + 1)
@@ -122,8 +124,8 @@ def tile_picked_ytcpcc_pace_p_kernel(
             for t in ts:
                 for h in range(2):
                     sig[t, h] = sb("sig%d_%d" % (t, h), [P, 2, HALF], F32, tag="sig%d_%d" % (t % 2, h))
-            for i in range(2):
-                for t in ts:
+            order = [(i, t) for i in range(2) for t in ts]
+            for i, t in order:
                     for h in range(2):
                         bank = psum.tile([P, HALF], F32, name="acc", tag="bank%d" % (4 * (t % 2) + 2 * h + i))
                         cols = slice((t % 2) * P, (t % 2 + 1) * P)
@@ -140,11 +142,15 @@ def tile_picked_ytcpcc_pace_p_kernel(
                         banks[i, t, h] = bank
             for t in ts:
                 for h in range(2):
-                    nc.scalar.activation(sig[t, h][:], sig[t, h][:], ACT.Ln, bias=LN_FLOOR)
-                    for i, dst in enumerate((btl, work)):
-                        nc.vector.scalar_tensor_tensor(
-                            dst[t][:, halves[h]], sig[t, h][:, i, :], -1.0, banks[i, t, h][:], ALU.mult, ALU.max
-                        )
+                    width = HALF // 2 if (t, h) == (0, 0) else HALF
+                    for c in range(0, HALF, width):
+                        part = sig[t, h][:, :, c : c + width]
+                        nc.scalar.activation(part, part, ACT.Ln, bias=LN_FLOOR)
+                        for i, dst in enumerate((btl, work)):
+                            nc.vector.scalar_tensor_tensor(
+                                dst[t][:, h * HALF + c : h * HALF + c + width], part[:, i, :], -1.0,
+                                banks[i, t, h][:, c : c + width], ALU.mult, ALU.max,
+                            )
 
         def queue(g):
             ts = (2 * g, 2 * g + 1)
@@ -163,10 +169,10 @@ def tile_picked_ytcpcc_pace_p_kernel(
             sl = shr_sb[:, h * COLS : (h + 1) * COLS]
             nc.vector.tensor_tensor(num[t][:, halves[h]], q5[t][:].indirect(sl), btl[t][:, halves[h]], ALU.mult)
 
-        back = {}
+        back, roots = {}, {}
 
-        def invert(t, h):
-            turned = psum.tile([P, HALF], F32, name="turned", tag="bank%d" % (2 * (t % 2) + h))
+        def turn(t, h):
+            turned = psum.tile([P, HALF], F32, name="turned", tag="bank%d" % (2 * h + t % 2))
             for c in range(HALF // P):
                 src = slice(h * HALF + c * P, h * HALF + (c + 1) * P)
                 dst = turned[:, c * P : (c + 1) * P]
@@ -174,37 +180,43 @@ def tile_picked_ytcpcc_pace_p_kernel(
                 nc.tensor.matmul(dst, q5[t][:, src], ident[:], start=False, stop=True, is_transpose=True)
             root = sb("root%d_%d" % (t, h), [P, HALF], F32)
             nc.scalar.activation(root[:], turned[:], ACT.Abs_reciprocal_sqrt)
+            roots[t, h] = root
+
+        def invert(t, h):
+            root = roots[t, h]
             nc.scalar.activation(root[:], root[:], ACT.Square)
-            back[t, h] = psum.tile([P, HALF], F32, name="back", tag="bank%d" % (4 + 2 * (t % 2) + h))
+            back[t, h] = psum.tile([P, HALF], F32, name="back", tag="bank%d" % (4 + 2 * h + t % 2))
             for c in range(HALF // P):
                 blk = slice(c * P, (c + 1) * P)
                 nc.tensor.transpose(back[t, h][:, blk], root[:, blk], ident[:])
 
         def paces(t, h):
             nc.vector.scalar_tensor_tensor(
-                pace[t // 2][:, t % 2, halves[h]], num[t][:, halves[h]], unit7[:, t : t + 1], back[t, h][:],
+                pace[t // 2, h][:, t % 2, :], num[t][:, halves[h]], unit7[:, t : t + 1], back[t, h][:],
                 ALU.mult, ALU.mult,
             )
 
-        def pair(g, h):
-            members = pace[g][:, :, halves[h]].rearrange("p t (v d) -> p d v t", d=2)
+        def pair(g, k):
+            c0, w = pieces[k]
+            members = pace[g, c0 // HALF][:, :, c0 % HALF : c0 % HALF + w].rearrange("p t (v d) -> p d v t", d=2)
             for d in range(2):
                 nc.vector.scalar_tensor_tensor(
-                    pairw[h][:, g, d, :, :], members[:, 1 - d, :, :], -3.0 / 7.0, members[:, d, :, :],
+                    pairw[k][:, g, d, :, :], members[:, 1 - d, :, :], -3.0 / 7.0, members[:, d, :, :],
                     ALU.mult, ALU.add,
                 )
 
-        def finish(h):
-            hid = sb("hid%d" % h, [P, HALF * PACK], BF16)
+        def finish(k):
+            c0, w = pieces[k]
+            hid = sb("hid%d" % k, [P, w * PACK], BF16)
             nc.vector.tensor_copy(
-                hid[:].bitcast(I32).rearrange("p (c g) -> p c g", g=2),
-                pairw[h][:].rearrange("p g d v t -> p (g d v t)").bitcast(I32).rearrange("p (g c) -> p c g", g=2),
+                hid[:].bitcast(I32).rearrange("p (c i g) -> p c g i", g=2, i=2),
+                pairw[k][:].rearrange("p g d v t -> p (g d v t)").bitcast(I32).rearrange("p (g c i) -> p c g i", g=2, i=2),
             )
-            codes = sb("hc%d" % h, [P, HALF], U32)
-            scales = sb("hs%d" % h, [P, HALF], U8)
+            codes = sb("hc%d" % k, [P, w], U32)
+            scales = sb("hs%d" % k, [P, w], U8)
             nc.vector.quantize_mx(out=codes[:].bitcast(FP8X4), scales=scales[:], in_=hid[:])
             for m in range(N // P):
-                bank = psum.tile([P, HALF], F32, name="acc_out", tag="bank%d" % (2 * h + m))
+                bank = psum.tile([P, w], F32, name="acc_out", tag="bank%d" % (2 * k + m))
                 cols = slice(m * P, (m + 1) * P)
                 nc.tensor.matmul_mx(
                     out=bank[:],
@@ -215,16 +227,35 @@ def tile_picked_ytcpcc_pace_p_kernel(
                     start=True,
                     stop=True,
                 )
-                res = sb("res%d_%d" % (h, m), [P, HALF], F32)
-                nc.scalar.copy(
-                    res[:].rearrange("p (v d) -> p v d", d=2), bank[:].rearrange("p (d v) -> p v d", d=2)
-                )
-                nc.sync.dma_start(out[cols, halves[h]], res[:])
+                res = sb("res%d_%d" % (k, m), [P, w], F32)
+                dst = res[:].rearrange("p (v d) -> p v d", d=2)
+                src = bank[:].rearrange("p (d v) -> p v d", d=2)
+                if k == len(pieces) - 1 and m == 1:
+                    nc.vector.tensor_copy(dst, src)
+                else:
+                    nc.scalar.copy(dst, src)
+                nc.sync.dma_start(out[cols, c0 : c0 + w], res[:])
 
         def each(f, g):
             for h in range(2):
                 for t in (2 * g, 2 * g + 1):
                     f(t, h)
+
+        def divide(g):
+            steps = [(t, h) for h in range(2) for t in (2 * g, 2 * g + 1)]
+            turn(*steps[0])
+            for n, (t, h) in enumerate(steps):
+                if n + 1 < len(steps):
+                    turn(*steps[n + 1])
+                invert(t, h)
+                paces(t, h)
+                if t % 2 == 1:
+                    mine = [k for k, (c0, w) in enumerate(pieces) if c0 // HALF == h]
+                    for k in mine:
+                        pair(g, k)
+                    if g == 1:
+                        for k in mine:
+                            finish(k)
 
         softplus(0)
         softplus(1)
@@ -232,16 +263,7 @@ def tile_picked_ytcpcc_pace_p_kernel(
         each(numerator, 0)
         each(shared_btl, 0)
         queue(1)
-        each(invert, 0)
+        divide(0)
         each(shared_btl, 1)
         each(numerator, 1)
-        each(paces, 0)
-        pair(0, 0)
-        pair(0, 1)
-        each(invert, 1)
-        for h in range(2):
-            paces(2, h)
-            paces(3, h)
-        for h in range(2):
-            pair(1, h)
-            finish(h)
+        divide(1)

@@ -208,9 +208,10 @@ def tile_picked_ytcpcc_pace_p_kernel(
         def finish(k):
             c0, w = pieces[k]
             hid = sb("hid%d" % k, [P, w * PACK], BF16)
-            nc.vector.tensor_copy(
-                hid[:].bitcast(I32).rearrange("p (c i g) -> p c g i", g=2, i=2),
-                pairw[k][:].rearrange("p g d v t -> p (g d v t)").bitcast(I32).rearrange("p (g c i) -> p c g i", g=2, i=2),
+            weave, word = (nc.scalar.copy, U32) if k == 0 else (nc.vector.tensor_copy, I32)
+            weave(
+                hid[:].bitcast(word).rearrange("p (c i g) -> p c g i", g=2, i=2),
+                pairw[k][:].rearrange("p g d v t -> p (g d v t)").bitcast(word).rearrange("p (g c i) -> p c g i", g=2, i=2),
             )
             codes = sb("hc%d" % k, [P, w], U32)
             scales = sb("hs%d" % k, [P, w], U8)

from contextlib import ExitStack

import concourse.mybir as mybir
from concourse.masks import make_identity

K, T, S, N, H = 512, 2048, 1024, 256, 512
FLOPS = 2 * K * H * S * 2 + 2 * H * N * S

F32 = mybir.dt.float32
BF16 = mybir.dt.bfloat16
I32 = mybir.dt.int32
U32 = mybir.dt.uint32
U16 = mybir.dt.uint16
U8 = mybir.dt.uint8
FP8X4 = mybir.dt.float8_e4m3fn_x4
ALU = mybir.AluOpType
ACT = mybir.ActivationFunctionType

P = 128
PACK = 4
HALF = 512
PAIRS = HALF // 2
COLS = HALF // 16
LN_FLOOR = 2.0 ** -60


def tile_picked_ytcpcc_pace_p_kernel(
    tc, x_words, x_scales, w1, w2, infl, unit, w3, offs, shr, out
):
    nc = tc.nc
    with ExitStack() as ctx:
        keep = ctx.enter_context(tc.tile_pool(name="keep", bufs=1))
        psum = ctx.enter_context(tc.psum_pool(name="psum", bufs=1))

        def sb(name, shape, dtype, tag=None):
            return keep.tile(shape, dtype, name=name, tag=tag or name, align_bytes=64)

        offs_sb = sb("offs_sb", [P, S // 16], U16)
        shr_sb = sb("shr_sb", [P, S // 16], U16)
        xw = sb("xw", [P, T], U32)
        xs = sb("xs", [P, T], U8)
        nc.vector.memset(xs[:].bitcast(I32), 0)
        nc.sync.dma_start(offs_sb[:], offs)
        nc.sync.dma_start(
            xw[:].bitcast(I32), x_words[0].rearrange("p n t -> p (n t)").bitcast(I32)
        )
        for q in range(4):
            nc.sync.dma_start(
                xs[32 * q : 32 * q + 4, :].bitcast(I32),
                x_scales[0][4 * q : 4 * q + 4, :].bitcast(I32),
            )
        w_raw = []
        for name, w in (("w1", w1), ("w2", w2)):
            raw = sb(name + "_raw", [P, PACK, H], F32)
            nc.sync.dma_start(raw[:], w.rearrange("(p j) c -> p j c", j=PACK))
            w_raw.append(raw)
        nc.sync.dma_start(shr_sb[:], shr)
        infl_rows = infl.rearrange("(p t) j -> p t j", t=PACK)
        infl_sb = []
        for t in range(PACK):
            tile = sb("infl%d" % t, [P, S], F32)
            nc.sync.dma_start(tile[:], infl_rows[:, t, :])
            infl_sb.append(tile)
        unit_sb = sb("unit_sb", [P, PACK], F32)
        nc.sync.dma_start(unit_sb[:], unit.rearrange("(p t) o -> p (t o)", t=PACK))
        w3_raw = sb("w3_raw", [P, PACK, N], F32)
        nc.sync.dma_start(w3_raw[:], w3.rearrange("(p j) c -> p j c", j=PACK))

        ident = sb("ident", [P, P], F32)
        make_identity(nc, ident[:])

        gw, gs = {}, {}
        w_codes, w_scales = {}, {}

        def pick(h):
            gw[h] = sb("gw%d" % h, [P, HALF], U32, tag="gw%d" % h)
            gs[h] = sb("gs%d" % h, [P, HALF], U8)
            sl = offs_sb[:, h * COLS : (h + 1) * COLS]
            nc.vector.tensor_copy(gw[h][:], xw[:].indirect(sl))
            nc.vector.tensor_copy(gs[h][:], xs[:].indirect(sl))

        def weights(i, g):
            tag = "gw1" if (i, g) == (0, 0) else "wg"
            grouped = sb("wg%d_%d" % (i, g), [P, 2 * P * PACK], BF16, tag=tag)
            nc.vector.tensor_copy(
                grouped[:].rearrange("p (t m j) -> p m j t", t=2, j=PACK),
                w_raw[i][:].rearrange("p j (m t) -> p m j t", t=PACK)[:, :, :, 2 * g : 2 * g + 2],
            )
            w_codes[i, g] = sb("wc%d_%d" % (i, g), [P, 2 * P], U32)
            w_scales[i, g] = sb("ws%d_%d" % (i, g), [P, 2 * P], U8)
            nc.vector.quantize_mx(out=w_codes[i, g][:].bitcast(FP8X4), scales=w_scales[i, g][:], in_=grouped[:])

        pick(0)
        weights(0, 0)
        pick(1)
        weights(1, 0)
        weights(0, 1)
        weights(1, 1)

        w3g = sb("w3g", [P, N * PACK], BF16)
        nc.vector.tensor_copy(
            w3g[:].rearrange("p (c i j) -> p c j i", i=4, j=PACK),
            w3_raw[:].rearrange("p j (c i) -> p c j i", i=4),
        )
        w3_codes = sb("w3c", [P, N], U32)
        w3_scales = sb("w3s", [P, N], U8)
        nc.vector.quantize_mx(out=w3_codes[:].bitcast(FP8X4), scales=w3_scales[:], in_=w3g[:])
        unit7 = sb("unit7", [P, PACK], F32)
        nc.vector.tensor_scalar_mul(unit7[:], unit_sb[:], 0.7)

        halves = [slice(h * HALF, (h + 1) * HALF) for h in range(2)]
        btl = [sb("btl%d" % t, [P, S], F32) for t in range(PACK)]
        q5 = [sb("q5_%d" % t, [P, S], F32) for t in range(PACK)]
        work = [sb("work%d" % t, [P, S], F32) for t in range(PACK)]
        num = [sb("num%d" % t, [P, S], F32) for t in range(PACK)]
        den = [sb("den%d" % t, [P, S], F32) for t in range(PACK)]
        pace = {(g, h): sb("pace%d_%d" % (g, h), [P, 2, HALF], F32) for g in range(2) for h in range(2)}
        pieces = ((0, 512), (512, 256), (768, 256))
        pairw = [sb("pairw%d" % k, [P, 2, 2, w // 2, 2], BF16) for k, (c0, w) in enumerate(pieces)]

        def softplus(g):
            ts = (2 * g, 2 * g + 1)
            banks, sig = {}, {}
            for t in ts:
                for h in range(2):
                    sig[t, h] = sb("sig%d_%d" % (t, h), [P, 2, HALF], F32, tag="sig%d_%d" % (t % 2, h))
            order = [(i, t) for i in range(2) for t in ts]
            for i, t in order:
                    for h in range(2):
                        bank = psum.tile([P, HALF], F32, name="acc", tag="bank%d" % (4 * (t % 2) + 2 * h + i))
                        cols = slice((t % 2) * P, (t % 2 + 1) * P)
                        nc.tensor.matmul_mx(
                            out=bank[:],
                            lhsT=w_codes[i, g][:, cols].bitcast(FP8X4),
                            lhsT_scale=w_scales[i, g][:, cols],
                            rhs=gw[h][:].bitcast(FP8X4),
                            rhs_scale=gs[h][:],
                            start=True,
                            stop=True,
                        )
                        nc.scalar.activation(sig[t, h][:, i, :], bank[:], ACT.Sigmoid, scale=-1.0)
                        banks[i, t, h] = bank
            for t in ts:
                for h in range(2):
                    width = HALF // 2 if (t, h) == (0, 0) else HALF
                    for c in range(0, HALF, width):
                        part = sig[t, h][:, :, c : c + width]
                        nc.scalar.activation(part, part, ACT.Ln, bias=LN_FLOOR)
                        for i, dst in enumerate((btl, work)):
                            nc.vector.scalar_tensor_tensor(
                                dst[t][:, h * HALF + c : h * HALF + c + width], part[:, i, :], -1.0,
                                banks[i, t, h][:, c : c + width], ALU.mult, ALU.max,
                            )

        def queue(g):
            ts = (2 * g, 2 * g + 1)
            for t in ts:
                nc.vector.scalar_tensor_tensor(work[t][:], work[t][:], 0.3, btl[t][:], ALU.add, ALU.mult)
            for t in ts:
                nc.vector.scalar_tensor_tensor(work[t][:], work[t][:], -0.7, infl_sb[t][:], ALU.mult, ALU.add)
            for t in ts:
                nc.vector.tensor_scalar(q5[t][:], work[t][:], 0.0, 0.5, ALU.max, ALU.add)

        def shared_btl(t, h):
            sl = shr_sb[:, h * COLS : (h + 1) * COLS]
            nc.scalar.activation(den[t][:, halves[h]], btl[t][:].indirect(sl), ACT.Copy)

        def numerator(t, h):
            sl = shr_sb[:, h * COLS : (h + 1) * COLS]
            nc.vector.tensor_tensor(num[t][:, halves[h]], q5[t][:].indirect(sl), btl[t][:, halves[h]], ALU.mult)

        back, roots = {}, {}

        def turn(t, h):
            turned = psum.tile([P, HALF], F32, name="turned", tag="bank%d" % (2 * h + t % 2))
            for c in range(HALF // P):
                src = slice(h * HALF + c * P, h * HALF + (c + 1) * P)
                dst = turned[:, c * P : (c + 1) * P]
                nc.tensor.matmul(dst, den[t][:, src], ident[:], start=True, stop=False, is_transpose=True)
                nc.tensor.matmul(dst, q5[t][:, src], ident[:], start=False, stop=True, is_transpose=True)
            root = sb("root%d_%d" % (t, h), [P, HALF], F32)
            nc.scalar.activation(root[:], turned[:], ACT.Abs_reciprocal_sqrt)
            roots[t, h] = root

        def invert(t, h):
            root = roots[t, h]
            nc.scalar.activation(root[:], root[:], ACT.Square)
            back[t, h] = psum.tile([P, HALF], F32, name="back", tag="bank%d" % (4 + 2 * h + t % 2))
            for c in range(HALF // P):
                blk = slice(c * P, (c + 1) * P)
                nc.tensor.transpose(back[t, h][:, blk], root[:, blk], ident[:])

        def paces(t, h):
            nc.vector.scalar_tensor_tensor(
                pace[t // 2, h][:, t % 2, :], num[t][:, halves[h]], unit7[:, t : t + 1], back[t, h][:],
                ALU.mult, ALU.mult,
            )

        def pair(g, k):
            c0, w = pieces[k]
            members = pace[g, c0 // HALF][:, :, c0 % HALF : c0 % HALF + w].rearrange("p t (v d) -> p d v t", d=2)
            for d in range(2):
                nc.vector.scalar_tensor_tensor(
                    pairw[k][:, g, d, :, :], members[:, 1 - d, :, :], -3.0 / 7.0, members[:, d, :, :],
                    ALU.mult, ALU.add,
                )

        def finish(k):
            c0, w = pieces[k]
            hid = sb("hid%d" % k, [P, w * PACK], BF16)
            weave, word = (nc.scalar.copy, U32) if k == 0 else (nc.vector.tensor_copy, I32)
            weave(
                hid[:].bitcast(word).rearrange("p (c i g) -> p c g i", g=2, i=2),
                pairw[k][:].rearrange("p g d v t -> p (g d v t)").bitcast(word).rearrange("p (g c i) -> p c g i", g=2, i=2),
            )
            codes = sb("hc%d" % k, [P, w], U32)
            scales = sb("hs%d" % k, [P, w], U8)
            nc.vector.quantize_mx(out=codes[:].bitcast(FP8X4), scales=scales[:], in_=hid[:])
            for m in range(N // P):
                bank = psum.tile([P, w], F32, name="acc_out", tag="bank%d" % (2 * k + m))
                cols = slice(m * P, (m + 1) * P)
                nc.tensor.matmul_mx(
                    out=bank[:],
                    lhsT=w3_codes[:, cols].bitcast(FP8X4),
                    lhsT_scale=w3_scales[:, cols],
                    rhs=codes[:].bitcast(FP8X4),
                    rhs_scale=scales[:],
                    start=True,
                    stop=True,
                )
                res = sb("res%d_%d" % (k, m), [P, w], F32)
                dst = res[:].rearrange("p (v d) -> p v d", d=2)
                src = bank[:].rearrange("p (d v) -> p v d", d=2)
                if k == len(pieces) - 1 and m == 1:
                    nc.vector.tensor_copy(dst, src)
                else:
                    nc.scalar.copy(dst, src)
                nc.sync.dma_start(out[cols, c0 : c0 + w], res[:])

        def each(f, g):
            for h in range(2):
                for t in (2 * g, 2 * g + 1):
                    f(t, h)

        def divide(g):
            steps = [(t, h) for h in range(2) for t in (2 * g, 2 * g + 1)]
            turn(*steps[0])
            for n, (t, h) in enumerate(steps):
                if n + 1 < len(steps):
                    turn(*steps[n + 1])
                invert(t, h)
                paces(t, h)
                if t % 2 == 1:
                    mine = [k for k, (c0, w) in enumerate(pieces) if c0 // HALF == h]
                    for k in mine:
                        pair(g, k)
                    if g == 1:
                        for k in mine:
                            finish(k)

        softplus(0)
        softplus(1)
        queue(0)
        each(numerator, 0)
        each(shared_btl, 0)
        queue(1)
        divide(0)
        each(shared_btl, 1)
        each(numerator, 1)
        divide(1)
